import numpy as np
import ml_dtypes


def mxq(x, axis, fmt="e4m3"):
    dtype, down = {"e4m3": (ml_dtypes.float8_e4m3fn, 7), "e5m2": (ml_dtypes.float8_e5m2, 14)}[fmt]
    v = np.moveaxis(np.asarray(x, np.float32).astype(ml_dtypes.bfloat16).astype(np.float64), axis, -1)
    blocks = v.reshape(v.shape[:-1] + (-1, 32))
    amax = np.abs(blocks).max(-1, keepdims=True)
    byte = np.maximum(np.where(amax > 0, np.frexp(amax)[1] - 1 + 127, 0) - down, 1)
    scale = np.exp2(byte - 127.0)
    codes = (blocks / scale).astype(np.float32).astype(dtype).astype(np.float64)
    return np.moveaxis((codes * scale).reshape(v.shape), -1, axis)


WIDE = False


def mx_kscale(k):
    if not WIDE:
        return np.ones(k)
    levels = np.array([10, -10, 5, -5, 0])
    if k % 512:
        return np.exp2(np.random.permutation(np.resize(levels, k // 32))).repeat(32)
    a = np.empty((k // 512, 16))
    for p in range(k // 512):
        a[p, :8] = np.random.permutation(np.resize(levels, 8))
        for g in range(8):
            far = levels[np.abs(levels - a[p, g]) >= 10]
            a[p, g + 8] = far[np.random.randint(len(far))]
    return np.exp2(a.ravel()).repeat(32)


def f64(x):
    return np.asarray(x).astype(np.float64)


def striped(idx):
    return np.tile(np.asarray(idx).reshape(-1, 16).T, (8, 1)).astype(np.uint16)


def unstriped(offs):
    return offs[:16].T.reshape(-1).astype(np.int64)


E2M1 = np.array([0.0, 0.5, 1.0, 1.5, 2.0, 3.0, 4.0, 6.0, -0.0, -0.5, -1.0, -1.5, -2.0, -3.0, -4.0, -6.0])


def pack_weight(w, fmt):
    k, n = w.shape
    w = f64(np.asarray(w, np.float32).astype(ml_dtypes.bfloat16)).reshape(k // 32, 32, n)
    amax = np.abs(w).max(1)
    if fmt == "e4m3":
        byte = np.frexp(amax)[1] - 1 + 127 - 7
    else:
        mant, ex = np.frexp(amax / 6.0)
        byte = np.where(mant > 0.5, ex, ex - 1) + 127
    byte = np.clip(np.where(amax > 0, byte, 1), 1, 254)
    scaled = (w * np.exp2(127.0 - byte)[:, None, :]).reshape(k, n).astype(np.float32)
    by_word = np.ascontiguousarray(scaled.reshape(k // 512, 128, 4, n).transpose(0, 1, 3, 2))
    if fmt == "e4m3":
        words = by_word.astype(ml_dtypes.float8_e4m3fn).view(np.uint8)
    else:
        c = by_word.astype(ml_dtypes.float4_e2m1fn).view(np.uint8) & 0xF
        words = (c[..., 0::2] | (c[..., 1::2] << 4)).reshape(k // 512, 128, 2 * n)
    return np.ascontiguousarray(words), np.ascontiguousarray(byte.astype(np.uint8).reshape(k // 512, 16, n))


def unpack_weight(words, scales, fmt):
    g, _, n = scales.shape
    words = np.ascontiguousarray(words).reshape(g, 128, n, -1)
    if fmt == "e4m3":
        vals = words.view(ml_dtypes.float8_e4m3fn).astype(np.float64)
    else:
        nib = np.empty((g, 128, n, 4), np.uint8)
        nib[..., 0::2] = words & 0xF
        nib[..., 1::2] = words >> 4
        vals = E2M1[nib]
    vals = vals * np.repeat(np.exp2(scales.astype(np.float64) - 127.0), 8, axis=1)[..., None]
    return vals.transpose(0, 1, 3, 2).reshape(g * 512, n)


def bf(x):
    return np.asarray(x, np.float32).astype(ml_dtypes.bfloat16)


def planes(Y):
    r, m = Y.shape
    b = f64(bf(Y)).reshape(r // 32, 32, m)
    amax = np.abs(b).max(1)
    byte = np.clip(np.where(amax > 0, np.frexp(amax)[1] - 1 + 127 - 7, 1), 1, 254)
    codes = (b * np.exp2(127.0 - byte)[:, None, :]).reshape(r, m).astype(np.float32).astype(ml_dtypes.float8_e4m3fn).view(np.uint8)
    words = codes.reshape(r // 512, 128, 4, m).transpose(0, 1, 3, 2)
    return np.ascontiguousarray(words), np.ascontiguousarray(byte.astype(np.uint8).reshape(r // 512, 16, m))


K, L, T, S, J, N = 512, 512, 512, 512, 512, 512


def setup_inputs():
    n = np.random.standard_normal
    idx = np.random.randint(0, T, J)
    idx2 = np.random.randint(0, S, J)
    fk = mx_kscale(K)
    fl = mx_kscale(L)
    xap = pack_weight(n((K, T)) / fk[:, None], "e4m3")
    xbp = pack_weight(n((L, S)) / fl[:, None], "e2m1")
    wbp = pack_weight(n((L, N)) * 1 / np.sqrt(L) * fl[:, None], "e4m3")
    return {
        "xa_words": xap[0],
        "xa_scales": xap[1],
        "wa": (n((K, N)) * 1 / np.sqrt(K) * fk[:, None]).astype(np.float32),
        "xb_words": xbp[0],
        "xb_scales": xbp[1],
        "wb_words": wbp[0],
        "wb_scales": wbp[1],
        "offs": striped(idx),
        "offs2": striped(idx2),
    }


def reference(xa_words, xa_scales, wa, xb_words, xb_scales, wb_words, wb_scales, offs, offs2):
    idx = unstriped(offs)
    idx2 = unstriped(offs2)
    xau = unpack_weight(xa_words, xa_scales, "e4m3")
    xbu = unpack_weight(xb_words, xb_scales, "e2m1")
    wbu = unpack_weight(wb_words, wb_scales, "e4m3")
    waq = mxq(f64(wa), 0, "e4m3")
    za = waq.T @ xau
    zb = wbu.T @ xbu
    u = za[:, idx] * zb[:, idx2]
    y = u / (1.0 + np.abs(za[:, idx]) + np.abs(zb[:, idx2]))
    words, scales = planes(y)
    return y, words, scales

@@ -1,0 +1,226 @@
+from contextlib import ExitStack
+
+import concourse.mybir as mybir
+from concourse.masks import make_identity
+
+F32 = mybir.dt.float32
+BF16 = mybir.dt.bfloat16
+I32 = mybir.dt.int32
+U32 = mybir.dt.uint32
+U16 = mybir.dt.uint16
+U8 = mybir.dt.uint8
+FP8X4 = mybir.dt.float8_e4m3fn_x4
+FP4X4 = mybir.dt.float4_e2m1fn_x4
+ACT = mybir.ActivationFunctionType
+ALU = mybir.AluOpType
+
+P = 128
+D = 512
+PACK = 4
+WINDOW_A = 704
+CHUNK = 128
+FLOPS = 2 * 2 * 512 * 512 * 512
+
+
+def load_scales(queues, plane, scales):
+    rows = scales[0].bitcast(I32)
+    for q in range(4):
+        queues[q].dma_start(
+            out=plane[32 * q : 32 * q + 32, :].bitcast(I32),
+            in_=rows[4 * q : 4 * q + 4, :].unsqueeze(0).broadcast_to([8, 4, 128]),
+        )
+
+
+def tile_list_cross_lookup_product_pl_kernel(
+    tc, xa_words, xa_scales, wa, xb_words, xb_scales, wb_words, wb_scales, offs, offs2, out_0, out_1, out_2
+):
+    nc = tc.nc
+    with ExitStack() as ctx:
+        lists = ctx.enter_context(tc.tile_pool(name="lists", bufs=1))
+        keep = ctx.enter_context(tc.tile_pool(name="keep", bufs=1))
+        work = ctx.enter_context(tc.tile_pool(name="work", bufs=1))
+        psum = ctx.enter_context(tc.psum_pool(name="psum", bufs=1))
+
+        list_a = lists.tile([P, D // 16], U16)
+        list_b = lists.tile([P, D // 16], U16)
+
+        wb_raw = keep.tile([P, D], U32, align_bytes=64)
+        wb_codes = keep.tile([P, D], U32, align_bytes=64, tag="wb_codes")
+        wb_plane_raw = keep.tile([P, D], U8, tag="plane_raw_then_ga")
+        wb_plane = keep.tile([P, D], U8, align_bytes=64)
+        xb_codes = keep.tile([P, 2 * D], U8, align_bytes=64, tag="xb_codes")
+        xb_plane = keep.tile([P, D], U8, align_bytes=64)
+        xa_codes = keep.tile([P, D], U32, align_bytes=64)
+        xa_plane = keep.tile([P, D], U8, align_bytes=64)
+        wa_codes = keep.tile([P, D], U32, align_bytes=64)
+        wa_plane = keep.tile([P, D], U8, align_bytes=64)
+        wa_bf = keep.tile([P, PACK * D], BF16, align_bytes=64)
+        wa_raw = [keep.tile([P, PACK, D // 2], F32, name="wa_raw%d" % h) for h in range(2)]
+        za = [keep.tile([P, WINDOW_A], F32, name="za%d" % t) for t in range(PACK)]
+        zb = [keep.tile([P, WINDOW_A], F32, name="zb%d" % t, tag="zb%d" % t) for t in range(PACK)]
+        y_codes = keep.tile([P, D], U32, align_bytes=64)
+        y_plane = keep.tile([P, D], U8, align_bytes=64)
+        warm = keep.tile([P, 8], F32)
+        ident = keep.tile([P, P], F32)
+
+        wa_rows = wa.rearrange("(p j) n -> p j n", j=PACK)
+        for h in range(2):
+            nc.sync.dma_start(out=wa_raw[h][:], in_=wa_rows[:, :, h * 256 : (h + 1) * 256])
+        load_scales([nc.scalar] * 4, xa_plane, xa_scales)
+        nc.sync.dma_start(out=xa_codes[:].bitcast(I32), in_=xa_words[0].rearrange("p n t -> p (n t)").bitcast(I32))
+        nc.sync.dma_start(out=wb_raw[:].bitcast(I32), in_=wb_words[0].rearrange("p n t -> p (n t)").bitcast(I32))
+        load_scales([nc.sync, nc.sync, nc.gpsimd, nc.gpsimd], wb_plane_raw, wb_scales)
+        nc.sync.dma_start(list_a[:], offs)
+        nc.sync.dma_start(out=xb_codes[:].bitcast(I32), in_=xb_words[0].bitcast(I32))
+        load_scales([nc.sync] * 4, xb_plane, xb_scales)
+        nc.sync.dma_start(list_b[:], offs2)
+
+        nc.vector.memset(warm[:], 1.0)
+        nc.scalar.activation(warm[:, 4:5], warm[:, 0:1], ACT.Abs_reciprocal_sqrt, bias=1.0)
+        for t in range(PACK):
+            nc.vector.memset(za[t][:, D:], 0.0)
+            nc.vector.memset(zb[t][:, D:], 0.0)
+        make_identity(nc, ident[:])
+
+        grouped = wa_bf[:].rearrange("p (t m j) -> p m j t", t=PACK, j=PACK)
+        halves = [wa_raw[h][:].rearrange("p j (m t) -> p m j t", t=PACK) for h in range(2)]
+        nc.vector.tensor_copy(out=grouped[:, 0:64], in_=halves[0])
+        nc.vector.tensor_copy(out=grouped[:, 64:128, :, 0:1], in_=halves[1][:, :, :, 0:1])
+        nc.vector.tensor_copy(out=grouped[:, 64:128, :, 1:2], in_=halves[1][:, :, :, 1:2])
+        nc.scalar.copy(out=grouped[:, 64:128, :, 2:4], in_=halves[1][:, :, :, 2:4])
+        for t in range(PACK):
+            cols = slice(t * P, (t + 1) * P)
+            nc.vector.quantize_mx(out=wa_codes[:, cols].bitcast(FP8X4), scales=wa_plane[:, cols], in_=wa_bf[:, t * D : (t + 1) * D])
+
+        nc.vector.tensor_copy(
+            out=wb_codes[:].bitcast(I32).rearrange("p (t g i) -> p g t i", t=PACK, i=4),
+            in_=wb_raw[:].bitcast(I32).rearrange("p (g i t) -> p g t i", t=PACK, i=4),
+        )
+        nc.vector.tensor_copy(
+            out=wb_plane[:].rearrange("p (t g i) -> p g t i", t=PACK, i=16),
+            in_=wb_plane_raw[:].rearrange("p (g i t) -> p g t i", t=PACK, i=16),
+        )
+        for t in range(PACK):
+            cols = slice(t * P, (t + 1) * P)
+            parts = [(slice(0, D), t, nc.scalar.copy)]
+            if t == 0:
+                parts = [(slice(0, D // 2), 7, nc.vector.tensor_copy), (slice(D // 2, D), 0, nc.scalar.copy)]
+            for entries, bank, copy_out in parts:
+                acc = psum.tile([P, entries.stop - entries.start], F32, name="acc_a", tag="bank%d" % bank)
+                nc.tensor.matmul_mx(
+                    out=acc[:], lhsT=wa_codes[:, cols].bitcast(FP8X4), lhsT_scale=wa_plane[:, cols],
+                    rhs=xa_codes[:, entries].bitcast(FP8X4), rhs_scale=xa_plane[:, entries], start=True, stop=True,
+                )
+                copy_out(out=za[t][:, entries], in_=acc[:])
+
+        for t in range(PACK):
+            cols = slice(t * P, (t + 1) * P)
+            acc = psum.tile([P, D], F32, name="acc_b", tag="bank%d" % (4 + t))
+            nc.tensor.matmul_mx(
+                out=acc[:], lhsT=wb_codes[:, cols].bitcast(FP8X4), lhsT_scale=wb_plane[:, cols],
+                rhs=xb_codes[:].bitcast(FP4X4), rhs_scale=xb_plane[:], start=True, stop=True,
+            )
+            nc.scalar.copy(out=zb[t][:, :D], in_=acc[:])
+
+        y_rows = out_0.rearrange("(p t) j -> p t j", t=PACK)
+        words_out = out_1[0].rearrange("p n t -> p (n t)").bitcast(I32)
+        y = keep.tile([P, PACK, D], F32)
+        last = PACK - 1
+        ga_tags = ["plane_raw_then_ga", "ga1", "zb0", "zb1"]
+        ga, gb, abs_a, abs_b, u, sums, root, recip = {}, {}, {}, {}, {}, {}, {}, {}
+        blocks = [slice(j0, j0 + P) for j0 in range(0, D, P)]
+
+        def fresh(kind, t):
+            return work.tile([P, D], F32, name="%s%d" % (kind, t))
+
+        def gather_a(t):
+            ga[t] = keep.tile([P, D], F32, name="ga%d" % t, tag=ga_tags[t])
+            nc.vector.tensor_copy(out=ga[t][:], in_=za[t][:].indirect(list_a[:]))
+
+        def gather_b(t):
+            gb[t] = fresh("gb", t)
+            if t != last:
+                nc.vector.tensor_copy(out=gb[t][:], in_=zb[t][:].indirect(list_b[:]))
+            else:
+                for js in blocks:
+                    nc.vector.tensor_copy(out=gb[t][:, js], in_=zb[t][:].indirect(list_b[:, js.start // 16 : js.stop // 16]))
+
+        def magnitude_a(t):
+            abs_a[t] = keep.tile([P, D], F32, align_bytes=64, name="abs_a%d" % t, tag=["wb_codes", "xb_codes", "abs_a2", "abs_a3"][t])
+            nc.scalar.activation(abs_a[t][:], ga[t][:], ACT.Abs)
+            if t != last:
+                sums[t] = psum.tile([P, D], F32, name="sums", tag="bank%d" % t)
+                for js in blocks:
+                    nc.tensor.matmul(sums[t][:, js], abs_a[t][:, js], ident[:], start=(js.start == 0), stop=False, is_transpose=True)
+
+        def magnitude_b(t):
+            abs_b[t] = fresh("abs_b", t)
+            if t != last:
+                nc.scalar.activation(abs_b[t][:], gb[t][:], ACT.Abs)
+            else:
+                for js in blocks:
+                    nc.scalar.activation(abs_b[t][:, js], gb[t][:, js], ACT.Abs)
+
+        def reciprocal(t):
+            for js in blocks:
+                nc.tensor.matmul(sums[t][:, js], abs_b[t][:, js], ident[:], start=False, stop=(js.stop == D), is_transpose=True)
+            root[t] = fresh("root", t)
+            nc.scalar.activation(root[t][:], sums[t][:], ACT.Abs_reciprocal_sqrt, bias=1.0)
+            turned = fresh("turned", t)
+            nc.scalar.activation(turned[:], root[t][:], ACT.Square)
+            recip[t] = psum.tile([P, D], F32, name="recip", tag="bank%d" % (4 + t))
+            for js in blocks:
+                nc.tensor.transpose(recip[t][:, js], turned[:, js], ident[:])
+
+        def product(t):
+            u[t] = fresh("u", t)
+            engine = nc.vector if t != last else nc.vector
+            engine.tensor_tensor(out=u[t][:], in0=ga[t][:], in1=gb[t][:], op=ALU.mult)
+
+        def result(t):
+            nc.vector.tensor_tensor(out=y[:, t, :], in0=u[t][:], in1=recip[t][:], op=ALU.mult)
+            nc.sync.dma_start(out=y_rows[:, t, :], in_=y[:, t, :])
+
+        gather_a(0)
+        gather_a(1)
+        for step in range(PACK + 1):
+            if step < PACK:
+                gather_b(step)
+            if 2 <= step + 1 < PACK:
+                gather_a(step + 1)
+            if step < PACK:
+                magnitude_a(step)
+            if 0 <= step - 1 < last:
+                reciprocal(step - 1)
+            if step < PACK:
+                magnitude_b(step)
+            if 0 <= step - 2 < last:
+                result(step - 2)
+            if 0 <= step - 1:
+                product(step - 1)
+
+        total = fresh("total", last)
+        root_last = fresh("root", last)
+        recip_last = fresh("recip", last)
+        for k, js in enumerate(blocks):
+            nc.vector.tensor_tensor(out=total[:, js], in0=abs_a[last][:, js], in1=abs_b[last][:, js], op=ALU.add)
+            nc.scalar.activation(root_last[:, js], total[:, js], ACT.Abs_reciprocal_sqrt, bias=1.0)
+            nc.scalar.activation(recip_last[:, js], root_last[:, js], ACT.Square)
+            nc.vector.tensor_tensor(out=y[:, last, js], in0=u[last][:, js], in1=recip_last[:, js], op=ALU.mult)
+            y_bf = work.tile([P, P * PACK], BF16, align_bytes=64, name="y_bf%d" % k)
+            y_in = y[:, :, js].rearrange("p t (c i) -> p c t i", i=4)
+            y_out = y_bf[:].rearrange("p (c i t) -> p c t i", t=PACK, i=4)
+            if k % 2 == 0:
+                nc.scalar.copy(out=y_out, in_=y_in)
+            else:
+                nc.vector.tensor_copy(out=y_out, in_=y_in)
+            nc.vector.quantize_mx(out=y_codes[:, js].bitcast(FP8X4), scales=y_plane[:, js], in_=y_bf[:])
+            if k % 2 == 1:
+                pair = slice(js.start - P, js.stop)
+                nc.sync.dma_start(out=y_rows[:, last, pair], in_=y[:, last, pair])
+                nc.sync.dma_start(out=words_out[:, pair], in_=y_codes[:, pair].bitcast(I32))
+
+        scale_rows = out_2[0].bitcast(I32)
+        for q in range(4):
+            queue = nc.sync if q % 2 == 0 else nc.scalar
+            queue.dma_start(out=scale_rows[4 * q : 4 * q + 4, :], in_=y_plane[32 * q : 32 * q + 4, :].bitcast(I32))

@@ -55,7 +55,7 @@ def tile_list_cross_lookup_product_pl_kernel(
         wa_codes = keep.tile([P, D], U32, align_bytes=64)
         wa_plane = keep.tile([P, D], U8, align_bytes=64)
         wa_bf = keep.tile([P, PACK * D], BF16, align_bytes=64)
-        wa_raw = [keep.tile([P, PACK, D // 2], F32, name="wa_raw%d" % h) for h in range(2)]
+        wa_raw = [keep.tile([P, 2, D], F32, name="wa_raw%d" % h) for h in range(2)]
         za = [keep.tile([P, WINDOW_A], F32, name="za%d" % t) for t in range(PACK)]
         zb = [keep.tile([P, WINDOW_A], F32, name="zb%d" % t, tag="zb%d" % t) for t in range(PACK)]
         y_codes = keep.tile([P, D], U32, align_bytes=64)
@@ -65,7 +65,7 @@ def tile_list_cross_lookup_product_pl_kernel(
 
         wa_rows = wa.rearrange("(p j) n -> p j n", j=PACK)
         for h in range(2):
-            nc.sync.dma_start(out=wa_raw[h][:], in_=wa_rows[:, :, h * 256 : (h + 1) * 256])
+            nc.sync.dma_start(out=wa_raw[h][:], in_=wa_rows[:, 2 * h : 2 * h + 2, :])
         load_scales([nc.scalar] * 4, xa_plane, xa_scales)
         nc.sync.dma_start(out=xa_codes[:].bitcast(I32), in_=xa_words[0].rearrange("p n t -> p (n t)").bitcast(I32))
         nc.sync.dma_start(out=wb_raw[:].bitcast(I32), in_=wb_words[0].rearrange("p n t -> p (n t)").bitcast(I32))
@@ -84,10 +84,9 @@ def tile_list_cross_lookup_product_pl_kernel(
 
         grouped = wa_bf[:].rearrange("p (t m j) -> p m j t", t=PACK, j=PACK)
         halves = [wa_raw[h][:].rearrange("p j (m t) -> p m j t", t=PACK) for h in range(2)]
-        nc.vector.tensor_copy(out=grouped[:, 0:64], in_=halves[0])
-        nc.vector.tensor_copy(out=grouped[:, 64:128, :, 0:1], in_=halves[1][:, :, :, 0:1])
-        nc.vector.tensor_copy(out=grouped[:, 64:128, :, 1:2], in_=halves[1][:, :, :, 1:2])
-        nc.scalar.copy(out=grouped[:, 64:128, :, 2:4], in_=halves[1][:, :, :, 2:4])
+        nc.vector.tensor_copy(out=grouped[:, :, 0:2, :], in_=halves[0])
+        nc.vector.tensor_copy(out=grouped[:, :, 2:4, 0:2], in_=halves[1][:, :, :, 0:2])
+        nc.scalar.copy(out=grouped[:, :, 2:4, 2:4], in_=halves[1][:, :, :, 2:4])
         for t in range(PACK):
             cols = slice(t * P, (t + 1) * P)
             nc.vector.quantize_mx(out=wa_codes[:, cols].bitcast(FP8X4), scales=wa_plane[:, cols], in_=wa_bf[:, t * D : (t + 1) * D])
@@ -126,7 +125,7 @@ def tile_list_cross_lookup_product_pl_kernel(
         words_out = out_1[0].rearrange("p n t -> p (n t)").bitcast(I32)
         y = keep.tile([P, PACK, D], F32)
         last = PACK - 1
-        ga_tags = ["plane_raw_then_ga", "ga1", "zb0", "zb1"]
+        ga_tags = ["plane_raw_then_ga", "ga1", "zb1", "zb2"]
         ga, gb, abs_a, abs_b, u, sums, root, recip = {}, {}, {}, {}, {}, {}, {}, {}
         blocks = [slice(j0, j0 + P) for j0 in range(0, D, P)]
 
@@ -174,7 +173,7 @@ def tile_list_cross_lookup_product_pl_kernel(
 
         def product(t):
             u[t] = fresh("u", t)
-            engine = nc.vector if t != last else nc.vector
+            engine = nc.gpsimd if t != last else nc.vector
             engine.tensor_tensor(out=u[t][:], in0=ga[t][:], in1=gb[t][:], op=ALU.mult)
 
         def result(t):

@@ -26,8 +26,8 @@ def load_scales(queues, plane, scales):
     rows = scales[0].bitcast(I32)
     for q in range(4):
         queues[q].dma_start(
-            out=plane[32 * q : 32 * q + 32, :].bitcast(I32),
-            in_=rows[4 * q : 4 * q + 4, :].unsqueeze(0).broadcast_to([8, 4, 128]),
+            out=plane[32 * q : 32 * q + 4, :].bitcast(I32),
+            in_=rows[4 * q : 4 * q + 4, :],
         )
 
 
@@ -56,13 +56,14 @@ def tile_list_cross_lookup_product_pl_kernel(
         wa_plane = keep.tile([P, D], U8, align_bytes=64)
         wa_bf = keep.tile([P, PACK * D], BF16, align_bytes=64)
         wa_raw = [keep.tile([P, 2, D], F32, name="wa_raw%d" % h) for h in range(2)]
-        za = [keep.tile([P, WINDOW_A], F32, name="za%d" % t) for t in range(PACK)]
+        za = [keep.tile([P, WINDOW_A], F32, name="za%d" % t, tag="za%d" % t) for t in range(PACK)]
         zb = [keep.tile([P, WINDOW_A], F32, name="zb%d" % t, tag="zb%d" % t) for t in range(PACK)]
         y_codes = keep.tile([P, D], U32, align_bytes=64)
         y_plane = keep.tile([P, D], U8, align_bytes=64)
         warm = keep.tile([P, 8], F32)
         ident = keep.tile([P, P], F32)
 
+        nc.gpsimd.memset(wb_plane_raw[:].bitcast(I32), 0)
         wa_rows = wa.rearrange("(p j) n -> p j n", j=PACK)
         for h in range(2):
             nc.sync.dma_start(out=wa_raw[h][:], in_=wa_rows[:, 2 * h : 2 * h + 2, :])
@@ -125,8 +126,10 @@ def tile_list_cross_lookup_product_pl_kernel(
         words_out = out_1[0].rearrange("p n t -> p (n t)").bitcast(I32)
         y = keep.tile([P, PACK, D], F32)
         last = PACK - 1
-        ga_tags = ["plane_raw_then_ga", "ga1", "zb1", "zb2"]
+        ga_tags = ["plane_raw_then_ga", "ga1", "zb1", "za2"]
         ga, gb, abs_a, abs_b, u, sums, root, recip = {}, {}, {}, {}, {}, {}, {}, {}
+        halves_j = [slice(0, D // 2), slice(D // 2, D)]
+        turned_slices = 2
         blocks = [slice(j0, j0 + P) for j0 in range(0, D, P)]
 
         def fresh(kind, t):
@@ -137,17 +140,17 @@ def tile_list_cross_lookup_product_pl_kernel(
             nc.vector.tensor_copy(out=ga[t][:], in_=za[t][:].indirect(list_a[:]))
 
         def gather_b(t):
-            gb[t] = fresh("gb", t)
+            gb[t] = keep.tile([P, D], F32, name="gb%d" % t, tag="zb2" if t == last else "gb%d" % t)
             if t != last:
                 nc.vector.tensor_copy(out=gb[t][:], in_=zb[t][:].indirect(list_b[:]))
             else:
-                for js in blocks:
+                for js in halves_j:
                     nc.vector.tensor_copy(out=gb[t][:, js], in_=zb[t][:].indirect(list_b[:, js.start // 16 : js.stop // 16]))
 
         def magnitude_a(t):
             abs_a[t] = keep.tile([P, D], F32, align_bytes=64, name="abs_a%d" % t, tag=["wb_codes", "xb_codes", "abs_a2", "abs_a3"][t])
             nc.scalar.activation(abs_a[t][:], ga[t][:], ACT.Abs)
-            if t != last:
+            if t < turned_slices:
                 sums[t] = psum.tile([P, D], F32, name="sums", tag="bank%d" % t)
                 for js in blocks:
                     nc.tensor.matmul(sums[t][:, js], abs_a[t][:, js], ident[:], start=(js.start == 0), stop=False, is_transpose=True)
@@ -157,10 +160,21 @@ def tile_list_cross_lookup_product_pl_kernel(
             if t != last:
                 nc.scalar.activation(abs_b[t][:], gb[t][:], ACT.Abs)
             else:
-                for js in blocks:
-                    nc.scalar.activation(abs_b[t][:, js], gb[t][:, js], ACT.Abs)
+                first, second = halves_j
+                nc.vector.scalar_tensor_tensor(
+                    out=abs_b[t][:, first], in0=gb[t][:, first], scalar=-1.0, in1=gb[t][:, first], op0=ALU.mult, op1=ALU.max
+                )
+                nc.scalar.activation(abs_b[t][:, second], gb[t][:, second], ACT.Abs)
 
         def reciprocal(t):
+            if t >= turned_slices:
+                sums[t] = fresh("sums", t)
+                nc.gpsimd.tensor_tensor(out=sums[t][:], in0=abs_a[t][:], in1=abs_b[t][:], op=ALU.add)
+                root[t] = fresh("root", t)
+                nc.scalar.activation(root[t][:], sums[t][:], ACT.Abs_reciprocal_sqrt, bias=1.0)
+                recip[t] = fresh("recip", t)
+                nc.scalar.activation(recip[t][:], root[t][:], ACT.Square)
+                return
             for js in blocks:
                 nc.tensor.matmul(sums[t][:, js], abs_b[t][:, js], ident[:], start=False, stop=(js.stop == D), is_transpose=True)
             root[t] = fresh("root", t)
@@ -201,23 +215,19 @@ def tile_list_cross_lookup_product_pl_kernel(
         total = fresh("total", last)
         root_last = fresh("root", last)
         recip_last = fresh("recip", last)
-        for k, js in enumerate(blocks):
+        for k, js in enumerate(halves_j):
             nc.vector.tensor_tensor(out=total[:, js], in0=abs_a[last][:, js], in1=abs_b[last][:, js], op=ALU.add)
             nc.scalar.activation(root_last[:, js], total[:, js], ACT.Abs_reciprocal_sqrt, bias=1.0)
             nc.scalar.activation(recip_last[:, js], root_last[:, js], ACT.Square)
             nc.vector.tensor_tensor(out=y[:, last, js], in0=u[last][:, js], in1=recip_last[:, js], op=ALU.mult)
-            y_bf = work.tile([P, P * PACK], BF16, align_bytes=64, name="y_bf%d" % k)
+            nc.sync.dma_start(out=y_rows[:, last, js], in_=y[:, last, js])
+            y_bf = work.tile([P, D // 2 * PACK], BF16, align_bytes=64, name="y_bf%d" % k)
             y_in = y[:, :, js].rearrange("p t (c i) -> p c t i", i=4)
             y_out = y_bf[:].rearrange("p (c i t) -> p c t i", t=PACK, i=4)
-            if k % 2 == 0:
-                nc.scalar.copy(out=y_out, in_=y_in)
-            else:
-                nc.vector.tensor_copy(out=y_out, in_=y_in)
+            nc.scalar.copy(out=y_out[:, 40:64], in_=y_in[:, 40:64])
+            nc.vector.tensor_copy(out=y_out[:, 0:40], in_=y_in[:, 0:40])
             nc.vector.quantize_mx(out=y_codes[:, js].bitcast(FP8X4), scales=y_plane[:, js], in_=y_bf[:])
-            if k % 2 == 1:
-                pair = slice(js.start - P, js.stop)
-                nc.sync.dma_start(out=y_rows[:, last, pair], in_=y[:, last, pair])
-                nc.sync.dma_start(out=words_out[:, pair], in_=y_codes[:, pair].bitcast(I32))
+            nc.sync.dma_start(out=words_out[:, js], in_=y_codes[:, js].bitcast(I32))
 
         scale_rows = out_2[0].bitcast(I32)
         for q in range(4):

@@ -22,12 +22,12 @@ CHUNK = 128
 FLOPS = 2 * 2 * 512 * 512 * 512
 
 
-def load_scales(queues, plane, scales):
+def load_scales(queues, plane, scales, repeats=1):
     rows = scales[0].bitcast(I32)
     for q in range(4):
         queues[q].dma_start(
-            out=plane[32 * q : 32 * q + 4, :].bitcast(I32),
-            in_=rows[4 * q : 4 * q + 4, :],
+            out=plane[32 * q : 32 * q + 4 * repeats, :].bitcast(I32),
+            in_=rows[4 * q : 4 * q + 4, :].unsqueeze(0).broadcast_to([repeats, 4, 128]),
         )
 
 
@@ -63,17 +63,16 @@ def tile_list_cross_lookup_product_pl_kernel(
         warm = keep.tile([P, 8], F32)
         ident = keep.tile([P, P], F32)
 
-        nc.gpsimd.memset(wb_plane_raw[:].bitcast(I32), 0)
         wa_rows = wa.rearrange("(p j) n -> p j n", j=PACK)
         for h in range(2):
             nc.sync.dma_start(out=wa_raw[h][:], in_=wa_rows[:, 2 * h : 2 * h + 2, :])
         load_scales([nc.scalar] * 4, xa_plane, xa_scales)
         nc.sync.dma_start(out=xa_codes[:].bitcast(I32), in_=xa_words[0].rearrange("p n t -> p (n t)").bitcast(I32))
         nc.sync.dma_start(out=wb_raw[:].bitcast(I32), in_=wb_words[0].rearrange("p n t -> p (n t)").bitcast(I32))
-        load_scales([nc.sync, nc.sync, nc.gpsimd, nc.gpsimd], wb_plane_raw, wb_scales)
+        load_scales([nc.sync, nc.sync, nc.gpsimd, nc.gpsimd], wb_plane_raw, wb_scales, repeats=8)
         nc.sync.dma_start(list_a[:], offs)
         nc.sync.dma_start(out=xb_codes[:].bitcast(I32), in_=xb_words[0].bitcast(I32))
-        load_scales([nc.sync] * 4, xb_plane, xb_scales)
+        load_scales([nc.sync, nc.sync, nc.gpsimd, nc.gpsimd], xb_plane, xb_scales)
         nc.sync.dma_start(list_b[:], offs2)
 
         nc.vector.memset(warm[:], 1.0)
@@ -126,6 +125,7 @@ def tile_list_cross_lookup_product_pl_kernel(
         words_out = out_1[0].rearrange("p n t -> p (n t)").bitcast(I32)
         y = keep.tile([P, PACK, D], F32)
         last = PACK - 1
+        ga_first = keep.tile([P, 2, D], F32, tag="plane_raw_then_ga")
         ga_tags = ["plane_raw_then_ga", "ga1", "zb1", "za2"]
         ga, gb, abs_a, abs_b, u, sums, root, recip = {}, {}, {}, {}, {}, {}, {}, {}
         halves_j = [slice(0, D // 2), slice(D // 2, D)]
@@ -136,7 +136,10 @@ def tile_list_cross_lookup_product_pl_kernel(
             return work.tile([P, D], F32, name="%s%d" % (kind, t))
 
         def gather_a(t):
-            ga[t] = keep.tile([P, D], F32, name="ga%d" % t, tag=ga_tags[t])
+            if t < 2:
+                ga[t] = ga_first[:, t, :]
+            else:
+                ga[t] = keep.tile([P, D], F32, name="ga%d" % t, tag=ga_tags[t])
             nc.vector.tensor_copy(out=ga[t][:], in_=za[t][:].indirect(list_a[:]))
 
         def gather_b(t):

from contextlib import ExitStack

import concourse.mybir as mybir
from concourse.masks import make_identity

F32 = mybir.dt.float32
BF16 = mybir.dt.bfloat16
I32 = mybir.dt.int32
U32 = mybir.dt.uint32
U16 = mybir.dt.uint16
U8 = mybir.dt.uint8
FP8X4 = mybir.dt.float8_e4m3fn_x4
FP4X4 = mybir.dt.float4_e2m1fn_x4
ACT = mybir.ActivationFunctionType
ALU = mybir.AluOpType

P = 128
D = 512
PACK = 4
WINDOW_A = 704
CHUNK = 128
FLOPS = 2 * 2 * 512 * 512 * 512


def load_scales(queues, plane, scales, repeats=1):
    rows = scales[0].bitcast(I32)
    for q in range(4):
        queues[q].dma_start(
            out=plane[32 * q : 32 * q + 4 * repeats, :].bitcast(I32),
            in_=rows[4 * q : 4 * q + 4, :].unsqueeze(0).broadcast_to([repeats, 4, 128]),
        )


def tile_list_cross_lookup_product_pl_kernel(
    tc, xa_words, xa_scales, wa, xb_words, xb_scales, wb_words, wb_scales, offs, offs2, out_0, out_1, out_2
):
    nc = tc.nc
    with ExitStack() as ctx:
        lists = ctx.enter_context(tc.tile_pool(name="lists", bufs=1))
        keep = ctx.enter_context(tc.tile_pool(name="keep", bufs=1))
        work = ctx.enter_context(tc.tile_pool(name="work", bufs=1))
        psum = ctx.enter_context(tc.psum_pool(name="psum", bufs=1))

        list_a = lists.tile([P, D // 16], U16)
        list_b = lists.tile([P, D // 16], U16)

        wb_raw = keep.tile([P, D], U32, align_bytes=64)
        wb_codes = keep.tile([P, D], U32, align_bytes=64, tag="wb_codes")
        wb_plane_raw = keep.tile([P, D], U8, tag="plane_raw_then_ga")
        wb_plane = keep.tile([P, D], U8, align_bytes=64)
        xb_codes = keep.tile([P, 2 * D], U8, align_bytes=64, tag="xb_codes")
        xb_plane = keep.tile([P, D], U8, align_bytes=64)
        xa_codes = keep.tile([P, D], U32, align_bytes=64)
        xa_plane = keep.tile([P, D], U8, align_bytes=64)
        wa_codes = keep.tile([P, D], U32, align_bytes=64)
        wa_plane = keep.tile([P, D], U8, align_bytes=64)
        wa_bf = keep.tile([P, PACK * D], BF16, align_bytes=64)
        wa_raw = [keep.tile([P, 2, D], F32, name="wa_raw%d" % h) for h in range(2)]
        za = [keep.tile([P, WINDOW_A], F32, name="za%d" % t, tag="za%d" % t) for t in range(PACK)]
        zb = [keep.tile([P, WINDOW_A], F32, name="zb%d" % t, tag="zb%d" % t) for t in range(PACK)]
        y_codes = keep.tile([P, D], U32, align_bytes=64)
        y_plane = keep.tile([P, D], U8, align_bytes=64)
        warm = keep.tile([P, 8], F32)
        ident = keep.tile([P, P], F32)

        wa_rows = wa.rearrange("(p j) n -> p j n", j=PACK)
        for h in range(2):
            nc.sync.dma_start(out=wa_raw[h][:], in_=wa_rows[:, 2 * h : 2 * h + 2, :])
        load_scales([nc.scalar] * 4, xa_plane, xa_scales)
        nc.sync.dma_start(out=xa_codes[:].bitcast(I32), in_=xa_words[0].rearrange("p n t -> p (n t)").bitcast(I32))
        nc.sync.dma_start(out=wb_raw[:].bitcast(I32), in_=wb_words[0].rearrange("p n t -> p (n t)").bitcast(I32))
        load_scales([nc.sync, nc.sync, nc.gpsimd, nc.gpsimd], wb_plane_raw, wb_scales, repeats=8)
        nc.sync.dma_start(list_a[:], offs)
        nc.sync.dma_start(out=xb_codes[:].bitcast(I32), in_=xb_words[0].bitcast(I32))
        load_scales([nc.sync, nc.sync, nc.gpsimd, nc.gpsimd], xb_plane, xb_scales)
        nc.sync.dma_start(list_b[:], offs2)

        nc.vector.memset(warm[:], 1.0)
        nc.scalar.activation(warm[:, 4:5], warm[:, 0:1], ACT.Abs_reciprocal_sqrt, bias=1.0)
        for t in range(PACK):
            nc.vector.memset(za[t][:, D:], 0.0)
            nc.vector.memset(zb[t][:, D:], 0.0)
        make_identity(nc, ident[:])

        grouped = wa_bf[:].rearrange("p (t m j) -> p m j t", t=PACK, j=PACK)
        halves = [wa_raw[h][:].rearrange("p j (m t) -> p m j t", t=PACK) for h in range(2)]
        nc.vector.tensor_copy(out=grouped[:, :, 0:2, :], in_=halves[0])
        nc.vector.tensor_copy(out=grouped[:, :, 2:4, 0:2], in_=halves[1][:, :, :, 0:2])
        nc.scalar.copy(out=grouped[:, :, 2:4, 2:4], in_=halves[1][:, :, :, 2:4])
        for t in range(PACK):
            cols = slice(t * P, (t + 1) * P)
            nc.vector.quantize_mx(out=wa_codes[:, cols].bitcast(FP8X4), scales=wa_plane[:, cols], in_=wa_bf[:, t * D : (t + 1) * D])

        nc.vector.tensor_copy(
            out=wb_codes[:].bitcast(I32).rearrange("p (t g i) -> p g t i", t=PACK, i=4),
            in_=wb_raw[:].bitcast(I32).rearrange("p (g i t) -> p g t i", t=PACK, i=4),
        )
        nc.vector.tensor_copy(
            out=wb_plane[:].rearrange("p (t g i) -> p g t i", t=PACK, i=16),
            in_=wb_plane_raw[:].rearrange("p (g i t) -> p g t i", t=PACK, i=16),
        )
        for t in range(PACK):
            cols = slice(t * P, (t + 1) * P)
            parts = [(slice(0, D), t, nc.scalar.copy)]
            if t == 0:
                parts = [(slice(0, D // 2), 7, nc.vector.tensor_copy), (slice(D // 2, D), 0, nc.scalar.copy)]
            for entries, bank, copy_out in parts:
                acc = psum.tile([P, entries.stop - entries.start], F32, name="acc_a", tag="bank%d" % bank)
                nc.tensor.matmul_mx(
                    out=acc[:], lhsT=wa_codes[:, cols].bitcast(FP8X4), lhsT_scale=wa_plane[:, cols],
                    rhs=xa_codes[:, entries].bitcast(FP8X4), rhs_scale=xa_plane[:, entries], start=True, stop=True,
                )
                copy_out(out=za[t][:, entries], in_=acc[:])

        for t in range(PACK):
            cols = slice(t * P, (t + 1) * P)
            acc = psum.tile([P, D], F32, name="acc_b", tag="bank%d" % (4 + t))
            nc.tensor.matmul_mx(
                out=acc[:], lhsT=wb_codes[:, cols].bitcast(FP8X4), lhsT_scale=wb_plane[:, cols],
                rhs=xb_codes[:].bitcast(FP4X4), rhs_scale=xb_plane[:], start=True, stop=True,
            )
            nc.scalar.copy(out=zb[t][:, :D], in_=acc[:])

        y_rows = out_0.rearrange("(p t) j -> p t j", t=PACK)
        words_out = out_1[0].rearrange("p n t -> p (n t)").bitcast(I32)
        y = keep.tile([P, PACK, D], F32)
        last = PACK - 1
        ga_first = keep.tile([P, 2, D], F32, tag="plane_raw_then_ga")
        ga_tags = ["plane_raw_then_ga", "ga1", "zb1", "za2"]
        ga, gb, abs_a, abs_b, u, sums, root, recip = {}, {}, {}, {}, {}, {}, {}, {}
        halves_j = [slice(0, D // 2), slice(D // 2, D)]
        turned_slices = 2
        blocks = [slice(j0, j0 + P) for j0 in range(0, D, P)]

        def fresh(kind, t):
            return work.tile([P, D], F32, name="%s%d" % (kind, t))

        def gather_a(t):
            if t < 2:
                ga[t] = ga_first[:, t, :]
            else:
                ga[t] = keep.tile([P, D], F32, name="ga%d" % t, tag=ga_tags[t])
            nc.vector.tensor_copy(out=ga[t][:], in_=za[t][:].indirect(list_a[:]))

        def gather_b(t):
            gb[t] = keep.tile([P, D], F32, name="gb%d" % t, tag="zb2" if t == last else "gb%d" % t)
            if t != last:
                nc.vector.tensor_copy(out=gb[t][:], in_=zb[t][:].indirect(list_b[:]))
            else:
                for js in halves_j:
                    nc.vector.tensor_copy(out=gb[t][:, js], in_=zb[t][:].indirect(list_b[:, js.start // 16 : js.stop // 16]))

        def magnitude_a(t):
            abs_a[t] = keep.tile([P, D], F32, align_bytes=64, name="abs_a%d" % t, tag=["wb_codes", "xb_codes", "abs_a2", "abs_a3"][t])
            nc.scalar.activation(abs_a[t][:], ga[t][:], ACT.Abs)
            if t < turned_slices:
                sums[t] = psum.tile([P, D], F32, name="sums", tag="bank%d" % t)
                for js in blocks:
                    nc.tensor.matmul(sums[t][:, js], abs_a[t][:, js], ident[:], start=(js.start == 0), stop=False, is_transpose=True)

        def magnitude_b(t):
            abs_b[t] = fresh("abs_b", t)
            if t != last:
                nc.scalar.activation(abs_b[t][:], gb[t][:], ACT.Abs)
            else:
                first, second = halves_j
                nc.vector.scalar_tensor_tensor(
                    out=abs_b[t][:, first], in0=gb[t][:, first], scalar=-1.0, in1=gb[t][:, first], op0=ALU.mult, op1=ALU.max
                )
                nc.scalar.activation(abs_b[t][:, second], gb[t][:, second], ACT.Abs)

        def reciprocal(t):
            if t >= turned_slices:
                sums[t] = fresh("sums", t)
                nc.gpsimd.tensor_tensor(out=sums[t][:], in0=abs_a[t][:], in1=abs_b[t][:], op=ALU.add)
                root[t] = fresh("root", t)
                nc.scalar.activation(root[t][:], sums[t][:], ACT.Abs_reciprocal_sqrt, bias=1.0)
                recip[t] = fresh("recip", t)
                nc.scalar.activation(recip[t][:], root[t][:], ACT.Square)
                return
            for js in blocks:
                nc.tensor.matmul(sums[t][:, js], abs_b[t][:, js], ident[:], start=False, stop=(js.stop == D), is_transpose=True)
            root[t] = fresh("root", t)
            nc.scalar.activation(root[t][:], sums[t][:], ACT.Abs_reciprocal_sqrt, bias=1.0)
            turned = fresh("turned", t)
            nc.scalar.activation(turned[:], root[t][:], ACT.Square)
            recip[t] = psum.tile([P, D], F32, name="recip", tag="bank%d" % (4 + t))
            for js in blocks:
                nc.tensor.transpose(recip[t][:, js], turned[:, js], ident[:])

        def product(t):
            u[t] = fresh("u", t)
            engine = nc.gpsimd if t != last else nc.vector
            engine.tensor_tensor(out=u[t][:], in0=ga[t][:], in1=gb[t][:], op=ALU.mult)

        def result(t):
            nc.vector.tensor_tensor(out=y[:, t, :], in0=u[t][:], in1=recip[t][:], op=ALU.mult)
            nc.sync.dma_start(out=y_rows[:, t, :], in_=y[:, t, :])

        gather_a(0)
        gather_a(1)
        for step in range(PACK + 1):
            if step < PACK:
                gather_b(step)
            if 2 <= step + 1 < PACK:
                gather_a(step + 1)
            if step < PACK:
                magnitude_a(step)
            if 0 <= step - 1 < last:
                reciprocal(step - 1)
            if step < PACK:
                magnitude_b(step)
            if 0 <= step - 2 < last:
                result(step - 2)
            if 0 <= step - 1:
                product(step - 1)

        total = fresh("total", last)
        root_last = fresh("root", last)
        recip_last = fresh("recip", last)
        for k, js in enumerate(halves_j):
            nc.vector.tensor_tensor(out=total[:, js], in0=abs_a[last][:, js], in1=abs_b[last][:, js], op=ALU.add)
            nc.scalar.activation(root_last[:, js], total[:, js], ACT.Abs_reciprocal_sqrt, bias=1.0)
            nc.scalar.activation(recip_last[:, js], root_last[:, js], ACT.Square)
            nc.vector.tensor_tensor(out=y[:, last, js], in0=u[last][:, js], in1=recip_last[:, js], op=ALU.mult)
            nc.sync.dma_start(out=y_rows[:, last, js], in_=y[:, last, js])
            y_bf = work.tile([P, D // 2 * PACK], BF16, align_bytes=64, name="y_bf%d" % k)
            y_in = y[:, :, js].rearrange("p t (c i) -> p c t i", i=4)
            y_out = y_bf[:].rearrange("p (c i t) -> p c t i", t=PACK, i=4)
            nc.scalar.copy(out=y_out[:, 40:64], in_=y_in[:, 40:64])
            nc.vector.tensor_copy(out=y_out[:, 0:40], in_=y_in[:, 0:40])
            nc.vector.quantize_mx(out=y_codes[:, js].bitcast(FP8X4), scales=y_plane[:, js], in_=y_bf[:])
            nc.sync.dma_start(out=words_out[:, js], in_=y_codes[:, js].bitcast(I32))

        scale_rows = out_2[0].bitcast(I32)
        for q in range(4):
            queue = nc.sync if q % 2 == 0 else nc.scalar
            queue.dma_start(out=scale_rows[4 * q : 4 * q + 4, :], in_=y_plane[32 * q : 32 * q + 4, :].bitcast(I32))
